import numpy as np
import ml_dtypes


def mxq(x, axis, fmt="e4m3"):
    dtype, down = {"e4m3": (ml_dtypes.float8_e4m3fn, 7), "e5m2": (ml_dtypes.float8_e5m2, 14)}[fmt]
    v = np.moveaxis(np.asarray(x, np.float32).astype(ml_dtypes.bfloat16).astype(np.float64), axis, -1)
    blocks = v.reshape(v.shape[:-1] + (-1, 32))
    amax = np.abs(blocks).max(-1, keepdims=True)
    byte = np.maximum(np.where(amax > 0, np.frexp(amax)[1] - 1 + 127, 0) - down, 1)
    scale = np.exp2(byte - 127.0)
    codes = (blocks / scale).astype(np.float32).astype(dtype).astype(np.float64)
    return np.moveaxis((codes * scale).reshape(v.shape), -1, axis)


WIDE = False


def mx_kscale(k):
    if not WIDE:
        return np.ones(k)
    levels = np.array([10, -10, 5, -5, 0])
    if k % 512:
        return np.exp2(np.random.permutation(np.resize(levels, k // 32))).repeat(32)
    a = np.empty((k // 512, 16))
    for p in range(k // 512):
        a[p, :8] = np.random.permutation(np.resize(levels, 8))
        for g in range(8):
            far = levels[np.abs(levels - a[p, g]) >= 10]
            a[p, g + 8] = far[np.random.randint(len(far))]
    return np.exp2(a.ravel()).repeat(32)


def f64(x):
    return np.asarray(x).astype(np.float64)


E2M1 = np.array([0.0, 0.5, 1.0, 1.5, 2.0, 3.0, 4.0, 6.0, -0.0, -0.5, -1.0, -1.5, -2.0, -3.0, -4.0, -6.0])


def pack_weight(w, fmt):
    k, n = w.shape
    w = f64(np.asarray(w, np.float32).astype(ml_dtypes.bfloat16)).reshape(k // 32, 32, n)
    amax = np.abs(w).max(1)
    if fmt == "e4m3":
        byte = np.frexp(amax)[1] - 1 + 127 - 7
    else:
        mant, ex = np.frexp(amax / 6.0)
        byte = np.where(mant > 0.5, ex, ex - 1) + 127
    byte = np.clip(np.where(amax > 0, byte, 1), 1, 254)
    scaled = (w * np.exp2(127.0 - byte)[:, None, :]).reshape(k, n).astype(np.float32)
    by_word = np.ascontiguousarray(scaled.reshape(k // 512, 128, 4, n).transpose(0, 1, 3, 2))
    if fmt == "e4m3":
        words = by_word.astype(ml_dtypes.float8_e4m3fn).view(np.uint8)
    else:
        c = by_word.astype(ml_dtypes.float4_e2m1fn).view(np.uint8) & 0xF
        words = (c[..., 0::2] | (c[..., 1::2] << 4)).reshape(k // 512, 128, 2 * n)
    return np.ascontiguousarray(words), np.ascontiguousarray(byte.astype(np.uint8).reshape(k // 512, 16, n))


def unpack_weight(words, scales, fmt):
    g, _, n = scales.shape
    words = np.ascontiguousarray(words).reshape(g, 128, n, -1)
    if fmt == "e4m3":
        vals = words.view(ml_dtypes.float8_e4m3fn).astype(np.float64)
    else:
        nib = np.empty((g, 128, n, 4), np.uint8)
        nib[..., 0::2] = words & 0xF
        nib[..., 1::2] = words >> 4
        vals = E2M1[nib]
    vals = vals * np.repeat(np.exp2(scales.astype(np.float64) - 127.0), 8, axis=1)[..., None]
    return vals.transpose(0, 1, 3, 2).reshape(g * 512, n)


K, M, T = 1024, 1024, 512


def setup_inputs():
    n = np.random.standard_normal
    s = mx_kscale(K)[:, None]
    u = mx_kscale(T)[:, None]
    q = n((K, T)) * s
    p_vc = pack_weight(0.1 * n((T, M)) / u, "e2m1")
    return {
        "qc": (q).astype(np.float32),
        "kc": (n((K, T)) / np.sqrt(K) / s).astype(np.float32),
        "qd": (q * 0.995 ** (np.arange(T) + 1.0)).astype(np.float32),
        "st": (n((K, M)) / np.sqrt(K) / s).astype(np.float32),
        "vc_words": p_vc[0],
        "vc_scales": p_vc[1],
        "dm": (np.tril(0.995 ** (np.arange(T)[:, None] - np.arange(T)[None])).T * u).astype(np.float32),
    }


def reference(qc, kc, qd, st, vc_words, vc_scales, dm):
    qc_ = mxq(f64(qc), 0, "e4m3")
    kc_ = mxq(f64(kc), 0, "e4m3")
    qd_ = mxq(f64(qd), 0, "e4m3")
    st_ = mxq(f64(st), 0, "e4m3")
    vc_ = unpack_weight(vc_words, vc_scales, "e2m1")
    h_ = mxq((kc_.T @ qc_) * f64(dm), 0, "e4m3")
    y = vc_.T @ h_ + st_.T @ qd_
    return y

@@ -1,0 +1,175 @@
+from contextlib import ExitStack
+
+import concourse.mybir as mybir
+
+K, M, T = 1024, 1024, 512
+FLOPS = 2 * K * T * T + 2 * T * M * T + 2 * K * M * T
+
+F32 = mybir.dt.float32
+BF16 = mybir.dt.bfloat16
+I32 = mybir.dt.int32
+U32 = mybir.dt.uint32
+U8 = mybir.dt.uint8
+FP8X4 = mybir.dt.float8_e4m3fn_x4
+FP4X4 = mybir.dt.float4_e2m1fn_x4
+MULT = mybir.AluOpType.mult
+
+P = 128
+PACK = 4
+K_PASS = P * PACK
+WIDE = 512
+HALF = WIDE // 2
+M_TILE = 128
+N_TILES = M // M_TILE
+CHUNK = 2 * M_TILE
+
+
+def tile_mix_linattn_fm_none_kernel(tc, qc, kc, qd, st, vc_words, vc_scales, dm, out):
+    nc = tc.nc
+    with ExitStack() as ctx:
+        sb = ctx.enter_context(tc.tile_pool(name="sb", bufs=1))
+        psum = ctx.enter_context(tc.psum_pool(name="psum", bufs=1))
+        ctx.enter_context(tc.manual_schedule())
+
+        def load_rows(name, rows):
+            raw = sb.tile([P, PACK, rows.shape[1]], F32, name=name)
+            nc.sync.dma_start(out=raw[:], in_=rows.rearrange("(p j) w -> p j w", j=PACK))
+            return raw
+
+        def copy_on(engine, dst, src):
+            if engine == "vector":
+                nc.vector.tensor_copy(out=dst, in_=src)
+            else:
+                nc.scalar.copy(out=dst, in_=src)
+
+        def interleave(engine, name, raw_cols):
+            width = raw_cols.shape[2]
+            grouped = sb.tile([P, width * PACK], BF16, name=name, align_bytes=64)
+            copy_on(
+                engine,
+                grouped[:].rearrange("p (c i j) -> p c j i", i=4, j=PACK),
+                raw_cols.rearrange("p j (c i) -> p c j i", i=4),
+            )
+            return grouped
+
+        def interleave_keys(engine, name, raw, first):
+            grouped = sb.tile([P, 2 * P * PACK], BF16, name=name, align_bytes=64)
+            copy_on(
+                engine,
+                grouped[:].rearrange("p (i m j) -> p m i j", i=2, j=PACK),
+                raw[:].rearrange("p j (m i) -> p m i j", i=PACK)[:, :, first : first + 2, :],
+            )
+            return grouped
+
+        def mx_tiles(name, width):
+            codes = sb.tile([P, width], U32, name=name + "_codes", align_bytes=64)
+            scales = sb.tile([P, width], U8, name=name + "_scales", align_bytes=64)
+            return codes, scales
+
+        def quantize(operand, col0, grouped):
+            codes, scales = operand
+            cols = slice(col0, col0 + grouped.shape[1] // PACK)
+            nc.vector.quantize_mx(out=codes[:, cols].bitcast(FP8X4), scales=scales[:, cols], in_=grouped[:])
+
+        def mx_pass(acc, stationary, col0, moving, start, stop):
+            cols = slice(col0, col0 + M_TILE)
+            nc.tensor.matmul_mx(
+                out=acc[:],
+                lhsT=stationary[0][:, cols].bitcast(FP8X4),
+                lhsT_scale=stationary[1][:, cols],
+                rhs=moving[0][:].bitcast(FP8X4),
+                rhs_scale=moving[1][:],
+                start=start,
+                stop=stop,
+            )
+
+        def prepare(name, raw, low_engine="scalar", high_engine="vector"):
+            operand = mx_tiles(name, WIDE)
+            low = interleave(low_engine, name + "_low", raw[:, :, :HALF])
+            high = interleave(high_engine, name + "_high", raw[:, :, HALF:])
+            quantize(operand, HALF, high)
+            quantize(operand, 0, low)
+            return operand
+
+        def prepare_keys(name, raw):
+            operand = mx_tiles(name, WIDE)
+            low = interleave_keys("scalar", name + "_low", raw, 0)
+            high = interleave_keys("vector", name + "_high", raw, 2)
+            quantize(operand, HALF, high)
+            quantize(operand, 0, low)
+            return operand
+
+        def rows_of(x, g):
+            return x[g * K_PASS : (g + 1) * K_PASS, :]
+
+        vc_plane = sb.tile([P, M], U8, align_bytes=64)
+        nc.gpsimd.memset(vc_plane[:].bitcast(U32), 0)
+        for q in range(4):
+            nc.gpsimd.dma_start(
+                out=vc_plane[32 * q : 32 * q + 4, :].bitcast(I32),
+                in_=vc_scales[0, 4 * q : 4 * q + 4, :].bitcast(I32),
+            )
+
+        kc_raw, qc_raw = [], []
+        for g in range(2):
+            kc_raw.append(load_rows("kc_raw%d" % g, rows_of(kc, g)))
+            qc_raw.append(load_rows("qc_raw%d" % g, rows_of(qc, g)))
+        dm_raw = load_rows("dm_raw", dm)
+        vc_codes = sb.tile([P, 2 * M], U8, align_bytes=64)
+        nc.sync.dma_start(out=vc_codes[:].bitcast(I32), in_=vc_words[0].bitcast(I32))
+        qd_raw = [load_rows("qd_raw%d" % g, rows_of(qd, g)) for g in range(2)]
+        st0_raw = [load_rows("st0_raw%d" % u, rows_of(st, 0)[:, u * WIDE : (u + 1) * WIDE]) for u in range(2)]
+        st1_raw = [
+            load_rows("st1_raw%d" % c, rows_of(st, 1)[:, c * CHUNK : (c + 1) * CHUNK]) for c in range(M // CHUNK)
+        ]
+
+        scores = [psum.tile([P, T], F32, name="scores%d" % i, tag="bank%d" % (4 + i)) for i in range(PACK)]
+        for g in range(2):
+            kc_mx = prepare_keys("kc%d" % g, kc_raw[g])
+            qc_mx = prepare("qc%d" % g, qc_raw[g])
+            for i in range(PACK):
+                mx_pass(scores[i], kc_mx, i * M_TILE, qc_mx, g == 0, g == 1)
+
+        h_rows = sb.tile([P, PACK, T], BF16, align_bytes=64)
+        for i in range(PACK):
+            nc.vector.tensor_tensor(out=h_rows[:, i, :], in0=scores[i][:], in1=dm_raw[:, i, :], op=MULT)
+        h_mx = mx_tiles("h", T)
+        h_low = interleave("vector", "h_low", h_rows[:, :, :HALF])
+        h_high = interleave("vector", "h_high", h_rows[:, :, HALF:])
+        quantize(h_mx, 0, h_low)
+        quantize(h_mx, HALF, h_high)
+
+        acc = [psum.tile([P, T], F32, name="acc%d" % n, tag="bank%d" % n) for n in range(N_TILES)]
+        for n in range(N_TILES):
+            nc.tensor.matmul_mx(
+                out=acc[n][:],
+                lhsT=vc_codes[:, 2 * n * M_TILE : 2 * (n + 1) * M_TILE].bitcast(FP4X4),
+                lhsT_scale=vc_plane[:, n * M_TILE : (n + 1) * M_TILE],
+                rhs=h_mx[0][:].bitcast(FP8X4),
+                rhs_scale=h_mx[1][:],
+                start=True,
+                stop=False,
+            )
+
+        qd_mx = [prepare("qd0", qd_raw[0], "scalar", "scalar"), prepare("qd1", qd_raw[1])]
+        for u in range(2):
+            st0_mx = prepare("st0_%d" % u, st0_raw[u])
+            for n in range(4):
+                mx_pass(acc[4 * u + n], st0_mx, n * M_TILE, qd_mx[0], False, False)
+
+        last = M // CHUNK - 1
+        for c in range(M // CHUNK):
+            st1_mx = mx_tiles("st1_%d" % c, CHUNK)
+            low = interleave("vector", "st1_low%d" % c, st1_raw[c][:, :, :M_TILE])
+            high = interleave("scalar" if c == 0 else "vector", "st1_high%d" % c, st1_raw[c][:, :, M_TILE:])
+            quantize(st1_mx, 0, low)
+            quantize(st1_mx, M_TILE, high)
+            result = sb.tile([P, 2, T], F32, name="result%d" % c)
+            rows = out[c * CHUNK : (c + 1) * CHUNK, :].rearrange("(a p) t -> p a t", p=P)
+            for a in range(2):
+                mx_pass(acc[2 * c + a], st1_mx, a * M_TILE, qd_mx[1], False, True)
+                copy_on("vector" if c == last and a == 1 else "scalar", result[:, a, :], acc[2 * c + a][:])
+                if c == last:
+                    nc.sync.dma_start(out=rows[:, a, :], in_=result[:, a, :])
+            if c != last:
+                nc.sync.dma_start(out=rows, in_=result[:])

@@ -21,7 +21,7 @@ WIDE = 512
 HALF = WIDE // 2
 M_TILE = 128
 N_TILES = M // M_TILE
-CHUNK = 2 * M_TILE
+ST_PIECES = [(0, 0, 4), (1, 0, 4), (0, 4, 2), (1, 4, 2), (0, 6, 2), (1, 6, 1), (1, 7, 1)]
 
 
 def tile_mix_linattn_fm_none_kernel(tc, qc, kc, qd, st, vc_words, vc_scales, dm, out):
@@ -104,24 +104,24 @@ def tile_mix_linattn_fm_none_kernel(tc, qc, kc, qd, st, vc_words, vc_scales, dm,
 
         vc_plane = sb.tile([P, M], U8, align_bytes=64)
         nc.gpsimd.memset(vc_plane[:].bitcast(U32), 0)
+
+        kc_raw = [load_rows("kc_raw0", rows_of(kc, 0))]
         for q in range(4):
-            nc.gpsimd.dma_start(
+            nc.sync.dma_start(
                 out=vc_plane[32 * q : 32 * q + 4, :].bitcast(I32),
                 in_=vc_scales[0, 4 * q : 4 * q + 4, :].bitcast(I32),
             )
-
-        kc_raw, qc_raw = [], []
-        for g in range(2):
-            kc_raw.append(load_rows("kc_raw%d" % g, rows_of(kc, g)))
-            qc_raw.append(load_rows("qc_raw%d" % g, rows_of(qc, g)))
+        qc_raw = [load_rows("qc_raw0", rows_of(qc, 0))]
+        kc_raw.append(load_rows("kc_raw1", rows_of(kc, 1)))
+        qc_raw.append(load_rows("qc_raw1", rows_of(qc, 1)))
         dm_raw = load_rows("dm_raw", dm)
         vc_codes = sb.tile([P, 2 * M], U8, align_bytes=64)
         nc.sync.dma_start(out=vc_codes[:].bitcast(I32), in_=vc_words[0].bitcast(I32))
         qd_raw = [load_rows("qd_raw%d" % g, rows_of(qd, g)) for g in range(2)]
-        st0_raw = [load_rows("st0_raw%d" % u, rows_of(st, 0)[:, u * WIDE : (u + 1) * WIDE]) for u in range(2)]
-        st1_raw = [
-            load_rows("st1_raw%d" % c, rows_of(st, 1)[:, c * CHUNK : (c + 1) * CHUNK]) for c in range(M // CHUNK)
-        ]
+        st_raw = {}
+        for g, first, count in ST_PIECES:
+            cols = slice(first * M_TILE, (first + count) * M_TILE)
+            st_raw[g, first] = load_rows("st_raw%d_%d" % (g, first), rows_of(st, g)[:, cols])
 
         scores = [psum.tile([P, T], F32, name="scores%d" % i, tag="bank%d" % (4 + i)) for i in range(PACK)]
         for g in range(2):
@@ -152,24 +152,32 @@ def tile_mix_linattn_fm_none_kernel(tc, qc, kc, qd, st, vc_words, vc_scales, dm,
             )
 
         qd_mx = [prepare("qd0", qd_raw[0], "scalar", "scalar"), prepare("qd1", qd_raw[1])]
-        for u in range(2):
-            st0_mx = prepare("st0_%d" % u, st0_raw[u])
-            for n in range(4):
-                mx_pass(acc[4 * u + n], st0_mx, n * M_TILE, qd_mx[0], False, False)
 
-        last = M // CHUNK - 1
-        for c in range(M // CHUNK):
-            st1_mx = mx_tiles("st1_%d" % c, CHUNK)
-            low = interleave("vector", "st1_low%d" % c, st1_raw[c][:, :, :M_TILE])
-            high = interleave("scalar" if c == 0 else "vector", "st1_high%d" % c, st1_raw[c][:, :, M_TILE:])
-            quantize(st1_mx, 0, low)
-            quantize(st1_mx, M_TILE, high)
-            result = sb.tile([P, 2, T], F32, name="result%d" % c)
-            rows = out[c * CHUNK : (c + 1) * CHUNK, :].rearrange("(a p) t -> p a t", p=P)
-            for a in range(2):
-                mx_pass(acc[2 * c + a], st1_mx, a * M_TILE, qd_mx[1], False, True)
-                copy_on("vector" if c == last and a == 1 else "scalar", result[:, a, :], acc[2 * c + a][:])
-                if c == last:
-                    nc.sync.dma_start(out=rows[:, a, :], in_=result[:, a, :])
-            if c != last:
-                nc.sync.dma_start(out=rows, in_=result[:])
+        def finish(first, count, engine):
+            result = sb.tile([P, count, T], F32, name="result%d" % first)
+            for a in range(count):
+                copy_on(engine, result[:, a, :], acc[first + a][:])
+            rows = out[first * M_TILE : (first + count) * M_TILE, :]
+            nc.sync.dma_start(out=rows.rearrange("(a p) t -> p a t", p=P), in_=result[:])
+
+        for g, first, count in ST_PIECES:
+            name = "st%d_%d" % (g, first)
+            raw = st_raw[g, first]
+            if count == 4:
+                st_mx = mx_tiles(name, WIDE)
+                low = interleave("vector", name + "_low", raw[:, :, :HALF])
+                high = interleave("scalar", name + "_high", raw[:, :, HALF:])
+                quantize(st_mx, 0, low)
+                quantize(st_mx, HALF, high)
+            else:
+                half = count * M_TILE // 2
+                st_mx = mx_tiles(name, count * M_TILE)
+                low = interleave("vector", name + "_low", raw[:, :, :half])
+                high = interleave("vector", name + "_high", raw[:, :, half:])
+                quantize(st_mx, 0, low)
+                quantize(st_mx, half, high)
+            for a in range(count):
+                mx_pass(acc[first + a], st_mx, a * M_TILE, qd_mx[g], False, g == 1)
+            if g == 1:
+                for pair in range(first, first + count, 2):
+                    finish(pair, min(count, 2), "vector" if first == N_TILES - 1 else "scalar")

from contextlib import ExitStack

import concourse.mybir as mybir

K, M, T = 1024, 1024, 512
FLOPS = 2 * K * T * T + 2 * T * M * T + 2 * K * M * T

F32 = mybir.dt.float32
BF16 = mybir.dt.bfloat16
I32 = mybir.dt.int32
U32 = mybir.dt.uint32
U8 = mybir.dt.uint8
FP8X4 = mybir.dt.float8_e4m3fn_x4
FP4X4 = mybir.dt.float4_e2m1fn_x4
MULT = mybir.AluOpType.mult

P = 128
PACK = 4
K_PASS = P * PACK
WIDE = 512
HALF = WIDE // 2
M_TILE = 128
N_TILES = M // M_TILE
ST_PIECES = [(0, 0, 4), (1, 0, 4), (0, 4, 2), (1, 4, 2), (0, 6, 2), (1, 6, 1), (1, 7, 1)]


def tile_mix_linattn_fm_none_kernel(tc, qc, kc, qd, st, vc_words, vc_scales, dm, out):
    nc = tc.nc
    with ExitStack() as ctx:
        sb = ctx.enter_context(tc.tile_pool(name="sb", bufs=1))
        psum = ctx.enter_context(tc.psum_pool(name="psum", bufs=1))
        ctx.enter_context(tc.manual_schedule())

        def load_rows(name, rows):
            raw = sb.tile([P, PACK, rows.shape[1]], F32, name=name)
            nc.sync.dma_start(out=raw[:], in_=rows.rearrange("(p j) w -> p j w", j=PACK))
            return raw

        def copy_on(engine, dst, src):
            if engine == "vector":
                nc.vector.tensor_copy(out=dst, in_=src)
            else:
                nc.scalar.copy(out=dst, in_=src)

        def interleave(engine, name, raw_cols):
            width = raw_cols.shape[2]
            grouped = sb.tile([P, width * PACK], BF16, name=name, align_bytes=64)
            copy_on(
                engine,
                grouped[:].rearrange("p (c i j) -> p c j i", i=4, j=PACK),
                raw_cols.rearrange("p j (c i) -> p c j i", i=4),
            )
            return grouped

        def interleave_keys(engine, name, raw, first):
            grouped = sb.tile([P, 2 * P * PACK], BF16, name=name, align_bytes=64)
            copy_on(
                engine,
                grouped[:].rearrange("p (i m j) -> p m i j", i=2, j=PACK),
                raw[:].rearrange("p j (m i) -> p m i j", i=PACK)[:, :, first : first + 2, :],
            )
            return grouped

        def mx_tiles(name, width):
            codes = sb.tile([P, width], U32, name=name + "_codes", align_bytes=64)
            scales = sb.tile([P, width], U8, name=name + "_scales", align_bytes=64)
            return codes, scales

        def quantize(operand, col0, grouped):
            codes, scales = operand
            cols = slice(col0, col0 + grouped.shape[1] // PACK)
            nc.vector.quantize_mx(out=codes[:, cols].bitcast(FP8X4), scales=scales[:, cols], in_=grouped[:])

        def mx_pass(acc, stationary, col0, moving, start, stop):
            cols = slice(col0, col0 + M_TILE)
            nc.tensor.matmul_mx(
                out=acc[:],
                lhsT=stationary[0][:, cols].bitcast(FP8X4),
                lhsT_scale=stationary[1][:, cols],
                rhs=moving[0][:].bitcast(FP8X4),
                rhs_scale=moving[1][:],
                start=start,
                stop=stop,
            )

        def prepare(name, raw, low_engine="scalar", high_engine="vector"):
            operand = mx_tiles(name, WIDE)
            low = interleave(low_engine, name + "_low", raw[:, :, :HALF])
            high = interleave(high_engine, name + "_high", raw[:, :, HALF:])
            quantize(operand, HALF, high)
            quantize(operand, 0, low)
            return operand

        def prepare_keys(name, raw):
            operand = mx_tiles(name, WIDE)
            low = interleave_keys("scalar", name + "_low", raw, 0)
            high = interleave_keys("vector", name + "_high", raw, 2)
            quantize(operand, HALF, high)
            quantize(operand, 0, low)
            return operand

        def rows_of(x, g):
            return x[g * K_PASS : (g + 1) * K_PASS, :]

        vc_plane = sb.tile([P, M], U8, align_bytes=64)
        nc.gpsimd.memset(vc_plane[:].bitcast(U32), 0)

        kc_raw = [load_rows("kc_raw0", rows_of(kc, 0))]
        for q in range(4):
            nc.sync.dma_start(
                out=vc_plane[32 * q : 32 * q + 4, :].bitcast(I32),
                in_=vc_scales[0, 4 * q : 4 * q + 4, :].bitcast(I32),
            )
        qc_raw = [load_rows("qc_raw0", rows_of(qc, 0))]
        kc_raw.append(load_rows("kc_raw1", rows_of(kc, 1)))
        qc_raw.append(load_rows("qc_raw1", rows_of(qc, 1)))
        dm_raw = load_rows("dm_raw", dm)
        vc_codes = sb.tile([P, 2 * M], U8, align_bytes=64)
        nc.sync.dma_start(out=vc_codes[:].bitcast(I32), in_=vc_words[0].bitcast(I32))
        qd_raw = [load_rows("qd_raw%d" % g, rows_of(qd, g)) for g in range(2)]
        st_raw = {}
        for g, first, count in ST_PIECES:
            cols = slice(first * M_TILE, (first + count) * M_TILE)
            st_raw[g, first] = load_rows("st_raw%d_%d" % (g, first), rows_of(st, g)[:, cols])

        scores = [psum.tile([P, T], F32, name="scores%d" % i, tag="bank%d" % (4 + i)) for i in range(PACK)]
        for g in range(2):
            kc_mx = prepare_keys("kc%d" % g, kc_raw[g])
            qc_mx = prepare("qc%d" % g, qc_raw[g])
            for i in range(PACK):
                mx_pass(scores[i], kc_mx, i * M_TILE, qc_mx, g == 0, g == 1)

        h_rows = sb.tile([P, PACK, T], BF16, align_bytes=64)
        for i in range(PACK):
            nc.vector.tensor_tensor(out=h_rows[:, i, :], in0=scores[i][:], in1=dm_raw[:, i, :], op=MULT)
        h_mx = mx_tiles("h", T)
        h_low = interleave("vector", "h_low", h_rows[:, :, :HALF])
        h_high = interleave("vector", "h_high", h_rows[:, :, HALF:])
        quantize(h_mx, 0, h_low)
        quantize(h_mx, HALF, h_high)

        acc = [psum.tile([P, T], F32, name="acc%d" % n, tag="bank%d" % n) for n in range(N_TILES)]
        for n in range(N_TILES):
            nc.tensor.matmul_mx(
                out=acc[n][:],
                lhsT=vc_codes[:, 2 * n * M_TILE : 2 * (n + 1) * M_TILE].bitcast(FP4X4),
                lhsT_scale=vc_plane[:, n * M_TILE : (n + 1) * M_TILE],
                rhs=h_mx[0][:].bitcast(FP8X4),
                rhs_scale=h_mx[1][:],
                start=True,
                stop=False,
            )

        qd_mx = [prepare("qd0", qd_raw[0], "scalar", "scalar"), prepare("qd1", qd_raw[1])]

        def finish(first, count, engine):
            result = sb.tile([P, count, T], F32, name="result%d" % first)
            for a in range(count):
                copy_on(engine, result[:, a, :], acc[first + a][:])
            rows = out[first * M_TILE : (first + count) * M_TILE, :]
            nc.sync.dma_start(out=rows.rearrange("(a p) t -> p a t", p=P), in_=result[:])

        for g, first, count in ST_PIECES:
            name = "st%d_%d" % (g, first)
            raw = st_raw[g, first]
            if count == 4:
                st_mx = mx_tiles(name, WIDE)
                low = interleave("vector", name + "_low", raw[:, :, :HALF])
                high = interleave("scalar", name + "_high", raw[:, :, HALF:])
                quantize(st_mx, 0, low)
                quantize(st_mx, HALF, high)
            else:
                half = count * M_TILE // 2
                st_mx = mx_tiles(name, count * M_TILE)
                low = interleave("vector", name + "_low", raw[:, :, :half])
                high = interleave("vector", name + "_high", raw[:, :, half:])
                quantize(st_mx, 0, low)
                quantize(st_mx, half, high)
            for a in range(count):
                mx_pass(acc[first + a], st_mx, a * M_TILE, qd_mx[g], False, g == 1)
            if g == 1:
                for pair in range(first, first + count, 2):
                    finish(pair, min(count, 2), "vector" if first == N_TILES - 1 else "scalar")
